import numpy as np
import ml_dtypes


def mxq(x, axis, fmt="e4m3"):
    dtype, down = {"e4m3": (ml_dtypes.float8_e4m3fn, 7), "e5m2": (ml_dtypes.float8_e5m2, 14)}[fmt]
    v = np.moveaxis(np.asarray(x, np.float32).astype(ml_dtypes.bfloat16).astype(np.float64), axis, -1)
    blocks = v.reshape(v.shape[:-1] + (-1, 32))
    amax = np.abs(blocks).max(-1, keepdims=True)
    byte = np.maximum(np.where(amax > 0, np.frexp(amax)[1] - 1 + 127, 0) - down, 1)
    scale = np.exp2(byte - 127.0)
    codes = (blocks / scale).astype(np.float32).astype(dtype).astype(np.float64)
    return np.moveaxis((codes * scale).reshape(v.shape), -1, axis)


WIDE = False


def mx_kscale(k):
    if not WIDE:
        return np.ones(k)
    levels = np.array([10, -10, 5, -5, 0])
    if k % 512:
        return np.exp2(np.random.permutation(np.resize(levels, k // 32))).repeat(32)
    a = np.empty((k // 512, 16))
    for p in range(k // 512):
        a[p, :8] = np.random.permutation(np.resize(levels, 8))
        for g in range(8):
            far = levels[np.abs(levels - a[p, g]) >= 10]
            a[p, g + 8] = far[np.random.randint(len(far))]
    return np.exp2(a.ravel()).repeat(32)


def f64(x):
    return np.asarray(x).astype(np.float64)


def striped(idx):
    return np.tile(idx.reshape(-1, 16).T, (8, 1)).astype(np.uint16)


def unstriped(offs):
    return offs[:16].T.reshape(-1).astype(np.int64)


def pack_weight(w):
    k, n = w.shape
    w = f64(np.asarray(w, np.float32).astype(ml_dtypes.bfloat16)).reshape(k // 32, 32, n)
    amax = np.abs(w).max(1)
    byte = np.clip(np.where(amax > 0, np.frexp(amax)[1] - 1 + 127 - 7, 1), 1, 254)
    scaled = (w * np.exp2(127.0 - byte)[:, None, :]).reshape(k, n).astype(np.float32)
    words = np.ascontiguousarray(scaled.reshape(k // 512, 128, 4, n).transpose(0, 1, 3, 2)).astype(ml_dtypes.float8_e4m3fn).view(np.uint8)
    return words, np.ascontiguousarray(byte.astype(np.uint8).reshape(k // 512, 16, n))


def unpack_weight(words, scales):
    g, p, n, _ = words.shape
    vals = np.ascontiguousarray(words).view(ml_dtypes.float8_e4m3fn).astype(np.float64) * np.repeat(np.exp2(scales.astype(np.float64) - 127.0), 8, axis=1)[..., None]
    return vals.transpose(0, 1, 3, 2).reshape(g * 512, n)


K, T, S, N = 512, 4096, 1024, 256


def setup_inputs():
    n = np.random.standard_normal
    s = mx_kscale(K)[:, None]
    packed_xT = pack_weight(n((K, T)) * s)
    return {
        "x_words": packed_xT[0],
        "x_scales": packed_xT[1],
        "w1": (n((K, N)) / np.sqrt(K) / s).astype(np.float32),
        "inc": (np.random.uniform(0.2, 3.0, (N, S))).astype(np.float32),
        "offs": striped(np.random.permutation(T)[:S]),
    }


def reference(x_words, x_scales, w1, inc, offs):
    xq = unpack_weight(x_words, x_scales)[:, unstriped(offs)]
    y = mxq(f64(w1), 0, "e4m3").T @ xq
    rep = 1.3 * (np.log(np.exp(y) + 1.0))
    mu = rep * (0.2 * (np.pad(f64(inc), ((0, 0), (1, 0)))[:, :S]) + 0.5 * (np.pad(f64(inc), ((0, 0), (2, 0)))[:, :S]) + 0.3 * (np.pad(f64(inc), ((0, 0), (3, 0)))[:, :S]))
    return 2.0 * (f64(inc) * (np.log((f64(inc) + 0.05) / (mu + 0.05))) - f64(inc) + mu)

@@ -1,0 +1,146 @@
+import math
+from contextlib import ExitStack
+
+import concourse.mybir as mybir
+
+K, T, S, N = 512, 4096, 1024, 256
+FLOPS = 2 * K * N * S
+
+F32 = mybir.dt.float32
+BF16 = mybir.dt.bfloat16
+I32 = mybir.dt.int32
+U32 = mybir.dt.uint32
+U16 = mybir.dt.uint16
+U8 = mybir.dt.uint8
+FP8X4 = mybir.dt.float8_e4m3fn_x4
+ALU = mybir.AluOpType
+ACT = mybir.ActivationFunctionType
+
+P = 128
+HALF = 512
+PAD = 8
+CAP = 32.0
+
+
+def tile_picked_yrenew_dev_p_kernel(tc, x_words, x_scales, w1, inc, offs, out):
+    nc = tc.nc
+    with ExitStack() as ctx:
+        keep = ctx.enter_context(tc.tile_pool(name="keep", bufs=1))
+        psum = ctx.enter_context(tc.psum_pool(name="psum", bufs=1))
+
+        offsets = keep.tile([P, S // 16], U16, name="offsets")
+        nc.sync.dma_start(offsets[:], offs)
+
+        scale_win = keep.tile([P, T], U8, name="scale_win", align_bytes=64)
+        nc.vector.memset(scale_win[:].bitcast(I32), 0)
+        for q in range(4):
+            nc.scalar.dma_start(
+                scale_win[32 * q : 32 * q + 4, :].bitcast(I32),
+                x_scales[0, 4 * q : 4 * q + 4, :].bitcast(I32),
+            )
+
+        seen = []
+        for h in range(2):
+            t = keep.tile([P, PAD + S], F32, name=f"seen{h}", align_bytes=64)
+            nc.vector.memset(t[:, 0:PAD], 0.0)
+            nc.sync.dma_start(t[:, PAD:], inc[h * P : (h + 1) * P, :])
+            seen.append(t)
+
+        w_raw = keep.tile([P, 4, N], F32, name="w_raw")
+        nc.sync.dma_start(w_raw[:], w1.rearrange("(p j) m -> p j m", j=4))
+
+        word_win = keep.tile([P, T], I32, name="word_win", align_bytes=64)
+        nc.sync.dma_start(word_win[:], x_words[0].rearrange("p n t -> p (n t)").bitcast(I32))
+
+        log_seen = []
+        for h in range(2):
+            t = keep.tile([P, S], F32, name=f"log_seen{h}")
+            nc.scalar.activation(t[:], seen[h][:, PAD:], ACT.Ln, bias=0.05 / math.e, scale=1.0 / math.e)
+            log_seen.append(t)
+
+        w_bf = keep.tile([P, N, 4], BF16, name="w_bf", align_bytes=64)
+        nc.scalar.copy(w_bf[:], w_raw[:].rearrange("p j m -> p m j"))
+
+        conv = []
+        for h in range(2):
+            part = keep.tile([P, S], F32, name=f"part{h}")
+            nc.vector.scalar_tensor_tensor(
+                part[:], seen[h][:, PAD - 2 : PAD - 2 + S], 2.5, seen[h][:, PAD - 1 : PAD - 1 + S], ALU.mult, ALU.add
+            )
+            conv.append(part)
+        picked_scales = keep.tile([P, S], U8, name="picked_scales", align_bytes=64)
+        nc.vector.tensor_copy(picked_scales[:], scale_win[:].indirect(offsets[:]))
+        for h in range(2):
+            full = keep.tile([P, S], F32, name=f"conv{h}")
+            nc.vector.scalar_tensor_tensor(
+                full[:], seen[h][:, PAD - 3 : PAD - 3 + S], 1.5, conv[h][:], ALU.mult, ALU.add
+            )
+            conv[h] = full
+
+        w_codes = keep.tile([P, N], U32, name="w_codes", align_bytes=64)
+        w_scales = keep.tile([P, N], U8, name="w_scales", align_bytes=64)
+        nc.vector.quantize_mx(w_codes[:].bitcast(FP8X4), w_scales[:], w_bf[:].rearrange("p m j -> p (m j)"))
+
+        picked = []
+        for d in range(2):
+            t = keep.tile([P, HALF], U32, name=f"picked{d}", align_bytes=64)
+            nc.vector.tensor_copy(
+                t[:], word_win[:].bitcast(U32).indirect(offsets[:, d * HALF // 16 : (d + 1) * HALF // 16])
+            )
+            picked.append(t)
+
+        chunks = [(h, d) for d in range(2) for h in range(2)]
+        grown = keep.tile([P, 4 * HALF], F32, name="grown")
+        gain = []
+        for c, (h, d) in enumerate(chunks):
+            y = psum.tile([P, HALF], F32, name=f"y{c}")
+            nc.tensor.matmul_mx(
+                y[:],
+                lhsT=w_codes[:, h * P : (h + 1) * P].bitcast(FP8X4),
+                lhsT_scale=w_scales[:, h * P : (h + 1) * P],
+                rhs=picked[d][:].bitcast(FP8X4),
+                rhs_scale=picked_scales[:, d * HALF : (d + 1) * HALF],
+                start=True,
+                stop=True,
+            )
+            nc.scalar.activation(grown[:, c * HALF : (c + 1) * HALF], y[:], ACT.Exp)
+            g = keep.tile([P, HALF], F32, name=f"gain{c}")
+            nc.vector.scalar_tensor_tensor(
+                g[:], y[:], CAP, conv[h][:, d * HALF : (d + 1) * HALF], ALU.max, ALU.mult
+            )
+            gain.append(g)
+
+        capped = keep.tile([P, 4 * HALF], F32, name="capped")
+        nc.vector.tensor_scalar_min(capped[:], grown[:], math.exp(CAP))
+
+        soft, mu2, log_mu, diff, term = {}, {}, {}, {}, {}
+
+        def stage(s, c):
+            h, d = chunks[c]
+            cols = slice(d * HALF, (d + 1) * HALF)
+            if s == 0:
+                soft[c] = keep.tile([P, HALF], F32, name=f"soft{c}")
+                nc.scalar.activation(soft[c][:], capped[:, c * HALF : (c + 1) * HALF], ACT.Ln, bias=1.0)
+                mu2[c] = keep.tile([P, HALF], F32, name=f"mu2_{c}")
+                nc.vector.scalar_tensor_tensor(
+                    mu2[c][:], soft[c][:], 2.0 * 1.3 * 0.2 / CAP, gain[c][:], ALU.mult, ALU.mult
+                )
+            elif s == 1:
+                log_mu[c] = keep.tile([P, HALF], F32, name=f"log_mu{c}")
+                nc.scalar.activation(log_mu[c][:], mu2[c][:], ACT.Ln, bias=0.05, scale=0.5)
+                diff[c] = keep.tile([P, HALF], F32, name=f"diff{c}")
+                nc.vector.tensor_sub(diff[c][:], log_seen[h][:, cols], log_mu[c][:])
+            elif s == 2:
+                term[c] = keep.tile([P, HALF], F32, name=f"term{c}")
+                nc.vector.scalar_tensor_tensor(
+                    term[c][:], diff[c][:], 2.0, seen[h][:, PAD + d * HALF : PAD + (d + 1) * HALF], ALU.mult, ALU.mult
+                )
+            else:
+                res = keep.tile([P, HALF], F32, name=f"res{c}")
+                nc.vector.tensor_add(res[:], term[c][:], mu2[c][:])
+                nc.sync.dma_start(out[h * P : (h + 1) * P, cols], res[:])
+
+        for step in range(4 + 3):
+            for s in range(4):
+                if 0 <= step - s < 4:
+                    stage(s, step - s)

@@ -2,6 +2,7 @@ import math
 from contextlib import ExitStack
 
 import concourse.mybir as mybir
+from concourse.masks import make_identity
 
 K, T, S, N = 512, 4096, 1024, 256
 FLOPS = 2 * K * N * S
@@ -18,6 +19,8 @@ ACT = mybir.ActivationFunctionType
 
 P = 128
 HALF = 512
+CH = 256
+NCH = S // CH
 PAD = 8
 CAP = 32.0
 
@@ -33,54 +36,81 @@ def tile_picked_yrenew_dev_p_kernel(tc, x_words, x_scales, w1, inc, offs, out):
 
         scale_win = keep.tile([P, T], U8, name="scale_win", align_bytes=64)
         nc.vector.memset(scale_win[:].bitcast(I32), 0)
+
+        one = keep.tile([P, 1], F32, name="one")
+        nc.gpsimd.memset(one[:], 1.0)
+        zero = keep.tile([P, 1], F32, name="zero")
+        nc.scalar.activation(zero[:], one[:], ACT.Ln)
+        ident = keep.tile([P, P], F32, name="ident")
+        make_identity(nc, ident[:])
+
+        seen = keep.tile([P, 2, PAD + S], F32, name="seen", align_bytes=64)
+        nc.vector.memset(seen[:, :, 0:PAD], 0.0)
+        inc_rows = inc.rearrange("(h p) j -> p h j", h=2)
+        for k in range(NCH):
+            nc.sync.dma_start(seen[:, :, PAD + k * CH : PAD + (k + 1) * CH], inc_rows[:, :, k * CH : (k + 1) * CH])
+
         for q in range(4):
-            nc.scalar.dma_start(
+            nc.sync.dma_start(
                 scale_win[32 * q : 32 * q + 4, :].bitcast(I32),
                 x_scales[0, 4 * q : 4 * q + 4, :].bitcast(I32),
             )
 
-        seen = []
-        for h in range(2):
-            t = keep.tile([P, PAD + S], F32, name=f"seen{h}", align_bytes=64)
-            nc.vector.memset(t[:, 0:PAD], 0.0)
-            nc.sync.dma_start(t[:, PAD:], inc[h * P : (h + 1) * P, :])
-            seen.append(t)
-
         w_raw = keep.tile([P, 4, N], F32, name="w_raw")
         nc.sync.dma_start(w_raw[:], w1.rearrange("(p j) m -> p j m", j=4))
 
-        word_win = keep.tile([P, T], I32, name="word_win", align_bytes=64)
+        word_win = keep.tile([P, T], I32, name="word_win", tag="word_win", align_bytes=64)
         nc.sync.dma_start(word_win[:], x_words[0].rearrange("p n t -> p (n t)").bitcast(I32))
 
-        log_seen = []
-        for h in range(2):
-            t = keep.tile([P, S], F32, name=f"log_seen{h}")
-            nc.scalar.activation(t[:], seen[h][:, PAD:], ACT.Ln, bias=0.05 / math.e, scale=1.0 / math.e)
-            log_seen.append(t)
+        def turned(b, h):
+            return slice(b * N + h * P, b * N + (h + 1) * P)
+
+        pair = keep.tile([P, 2, PAD + S], F32, name="pair", align_bytes=64)
+        seen_t, log_seen, conv = [], [], []
+        for k in range(NCH):
+            st = psum.tile([P, 2 * N], F32, name=f"seen_t{k}", tag=f"seen_t{k}")
+            for b in range(2):
+                for h in range(2):
+                    j0 = PAD + k * CH + b * P
+                    nc.tensor.transpose(st[:, turned(b, h)], seen[:, h, j0 : j0 + P], ident[:])
+            seen_t.append(st)
+            ls = keep.tile([P, 2 * N], F32, name=f"log_seen{k}")
+            nc.scalar.activation(ls[:], st[:], ACT.Ln, bias=0.05 / math.e, scale=1.0 / math.e)
+            log_seen.append(ls)
+
+            lo = PAD + k * CH - (1 if k == 0 else 0)
+            hi = PAD + (k + 1) * CH
+            nc.vector.scalar_tensor_tensor(
+                pair[:, :, lo:hi], seen[:, :, lo - 2 : hi - 2], 1.5, seen[:, :, lo - 1 : hi - 1], ALU.mult, ALU.add
+            )
+            ct = psum.tile([P, 2 * N], F32, name=f"conv_t{k}", tag=f"work{k}")
+            for b in range(2):
+                for h in range(2):
+                    j0 = PAD + k * CH + b * P
+                    for back in range(2):
+                        nc.tensor.matmul(
+                            ct[:, turned(b, h)],
+                            lhsT=pair[:, h, j0 - back : j0 - back + P],
+                            rhs=ident[:],
+                            is_transpose=True,
+                            start=(back == 0),
+                            stop=(back == 1),
+                        )
+            cs = keep.tile([P, 2 * N], F32, name=f"conv{k}")
+            nc.scalar.activation(cs[:], ct[:], ACT.Copy, scale=2.0 * 1.3 * 0.2 / CAP)
+            conv.append(cs)
 
         w_bf = keep.tile([P, N, 4], BF16, name="w_bf", align_bytes=64)
         nc.scalar.copy(w_bf[:], w_raw[:].rearrange("p j m -> p m j"))
-
-        conv = []
-        for h in range(2):
-            part = keep.tile([P, S], F32, name=f"part{h}")
-            nc.vector.scalar_tensor_tensor(
-                part[:], seen[h][:, PAD - 2 : PAD - 2 + S], 2.5, seen[h][:, PAD - 1 : PAD - 1 + S], ALU.mult, ALU.add
-            )
-            conv.append(part)
-        picked_scales = keep.tile([P, S], U8, name="picked_scales", align_bytes=64)
-        nc.vector.tensor_copy(picked_scales[:], scale_win[:].indirect(offsets[:]))
-        for h in range(2):
-            full = keep.tile([P, S], F32, name=f"conv{h}")
-            nc.vector.scalar_tensor_tensor(
-                full[:], seen[h][:, PAD - 3 : PAD - 3 + S], 1.5, conv[h][:], ALU.mult, ALU.add
-            )
-            conv[h] = full
-
         w_codes = keep.tile([P, N], U32, name="w_codes", align_bytes=64)
         w_scales = keep.tile([P, N], U8, name="w_scales", align_bytes=64)
         nc.vector.quantize_mx(w_codes[:].bitcast(FP8X4), w_scales[:], w_bf[:].rearrange("p m j -> p (m j)"))
 
+        exp_cap = keep.tile([P, 1], F32, name="exp_cap")
+        nc.scalar.activation(exp_cap[:], log_seen[NCH - 1][:, 0:1], ACT.Exp, bias=CAP, scale=0.0)
+
+        picked_scales = keep.tile([P, S], U8, name="picked_scales", align_bytes=64)
+        nc.vector.tensor_copy(picked_scales[:], scale_win[:].indirect(offsets[:]))
         picked = []
         for d in range(2):
             t = keep.tile([P, HALF], U32, name=f"picked{d}", align_bytes=64)
@@ -89,58 +119,106 @@ def tile_picked_yrenew_dev_p_kernel(tc, x_words, x_scales, w1, inc, offs, out):
             )
             picked.append(t)
 
-        chunks = [(h, d) for d in range(2) for h in range(2)]
-        grown = keep.tile([P, 4 * HALF], F32, name="grown")
-        gain = []
-        for c, (h, d) in enumerate(chunks):
-            y = psum.tile([P, HALF], F32, name=f"y{c}")
-            nc.tensor.matmul_mx(
-                y[:],
-                lhsT=w_codes[:, h * P : (h + 1) * P].bitcast(FP8X4),
-                lhsT_scale=w_scales[:, h * P : (h + 1) * P],
-                rhs=picked[d][:].bitcast(FP8X4),
-                rhs_scale=picked_scales[:, d * HALF : (d + 1) * HALF],
-                start=True,
-                stop=True,
-            )
-            nc.scalar.activation(grown[:, c * HALF : (c + 1) * HALF], y[:], ACT.Exp)
-            g = keep.tile([P, HALF], F32, name=f"gain{c}")
-            nc.vector.scalar_tensor_tensor(
-                g[:], y[:], CAP, conv[h][:, d * HALF : (d + 1) * HALF], ALU.max, ALU.mult
-            )
+        gain, capped = [], []
+        for k in range(NCH):
+            y = psum.tile([P, 2 * N], F32, name=f"y{k}", tag=f"work{k}")
+            for b in range(2):
+                j0 = k * CH + b * P
+                nc.tensor.matmul_mx(
+                    y[:, b * N : (b + 1) * N],
+                    lhsT=picked[j0 // HALF][:, j0 % HALF : j0 % HALF + P].bitcast(FP8X4),
+                    lhsT_scale=picked_scales[:, j0 : j0 + P],
+                    rhs=w_codes[:].bitcast(FP8X4),
+                    rhs_scale=w_scales[:],
+                    start=True,
+                    stop=True,
+                )
+            grown = keep.tile([P, 2 * N], F32, name=f"grown{k}")
+            nc.scalar.activation(grown[:], y[:], ACT.Exp, bias=zero[:])
+            cp = keep.tile([P, 2 * N], F32, name=f"capped{k}")
+            nc.gpsimd.tensor_scalar(cp[:], grown[:], exp_cap[:], 0.0, ALU.min, ALU.max)
+            capped.append(cp)
+            g = keep.tile([P, 2 * N], F32, name=f"gain{k}")
+            nc.vector.scalar_tensor_tensor(g[:], y[:], CAP, conv[k][:], ALU.max, ALU.mult)
             gain.append(g)
 
-        capped = keep.tile([P, 4 * HALF], F32, name="capped")
-        nc.vector.tensor_scalar_min(capped[:], grown[:], math.exp(CAP))
-
-        soft, mu2, log_mu, diff, term = {}, {}, {}, {}, {}
-
-        def stage(s, c):
-            h, d = chunks[c]
-            cols = slice(d * HALF, (d + 1) * HALF)
-            if s == 0:
-                soft[c] = keep.tile([P, HALF], F32, name=f"soft{c}")
-                nc.scalar.activation(soft[c][:], capped[:, c * HALF : (c + 1) * HALF], ACT.Ln, bias=1.0)
-                mu2[c] = keep.tile([P, HALF], F32, name=f"mu2_{c}")
-                nc.vector.scalar_tensor_tensor(
-                    mu2[c][:], soft[c][:], 2.0 * 1.3 * 0.2 / CAP, gain[c][:], ALU.mult, ALU.mult
-                )
-            elif s == 1:
-                log_mu[c] = keep.tile([P, HALF], F32, name=f"log_mu{c}")
-                nc.scalar.activation(log_mu[c][:], mu2[c][:], ACT.Ln, bias=0.05, scale=0.5)
-                diff[c] = keep.tile([P, HALF], F32, name=f"diff{c}")
-                nc.vector.tensor_sub(diff[c][:], log_seen[h][:, cols], log_mu[c][:])
-            elif s == 2:
-                term[c] = keep.tile([P, HALF], F32, name=f"term{c}")
-                nc.vector.scalar_tensor_tensor(
-                    term[c][:], diff[c][:], 2.0, seen[h][:, PAD + d * HALF : PAD + (d + 1) * HALF], ALU.mult, ALU.mult
-                )
+        late = keep.tile([P, 2, 2 * N], F32, name="own_late", tag="word_win", align_bytes=64)
+        own = []
+        for k in range(NCH):
+            if k < 2:
+                early = keep.tile([P, 2 * N], F32, name=f"own{k}")
+                o = early[:]
             else:
-                res = keep.tile([P, HALF], F32, name=f"res{c}")
-                nc.vector.tensor_add(res[:], term[c][:], mu2[c][:])
-                nc.sync.dma_start(out[h * P : (h + 1) * P, cols], res[:])
+                o = late[:, k - 2, :]
+            nc.vector.scalar_tensor_tensor(o, log_seen[k][:], 2.0, seen_t[k][:], ALU.mult, ALU.mult)
+            own.append(o)
 
-        for step in range(4 + 3):
-            for s in range(4):
-                if 0 <= step - s < 4:
-                    stage(s, step - s)
+        units = [(0, (0, 1), "work0"), (1, (0, 1), "work1"), (2, (0, 1), "work2"), (3, (0,), "work3"), (3, (1,), "seen_t0")]
+
+        def part(ap, u):
+            halves = units[u][1]
+            if len(halves) == 2:
+                return ap
+            return ap.rearrange("p (b h m) -> p b h m", b=2, h=2)[:, :, halves[0], :]
+
+        total = {}
+
+        def add_turned(u, term, first, last):
+            k, halves, tag = units[u]
+            if first:
+                total[u] = psum.tile([P, 2 * CH], F32, name=f"total{u}", tag=tag)
+            for i, h in enumerate(halves):
+                for b in range(2):
+                    nc.tensor.matmul(
+                        total[u][:, i * CH + b * P : i * CH + (b + 1) * P],
+                        lhsT=term[:, turned(b, h)],
+                        rhs=ident[:],
+                        is_transpose=True,
+                        start=(first and i == 0 and b == 0),
+                        stop=(last and i == len(halves) - 1 and b == 1),
+                    )
+
+        for u in range(4):
+            add_turned(u, own[units[u][0]], True, False)
+
+        out_rows = out.rearrange("(h p) j -> p h j", h=2)
+        mu2 = {}
+
+        def expected(k):
+            soft = keep.tile([P, 2 * N], F32, name=f"soft{k}")
+            nc.scalar.activation(soft[:], capped[k][:], ACT.Ln, bias=1.0)
+            mu2[k] = keep.tile([P, 2 * N], F32, name=f"mu2_{k}")
+            nc.vector.tensor_mul(mu2[k][:], soft[:], gain[k][:])
+            add_turned(k, mu2[k][:], False, False)
+
+        def cross_term(u):
+            k = units[u][0]
+            log_mu = keep.tile([P, 2 * N], F32, name=f"log_mu{u}")
+            nc.scalar.activation(part(log_mu[:], u), part(mu2[k][:], u), ACT.Ln, bias=0.05, scale=0.5)
+            cross = keep.tile([P, 2 * N], F32, name=f"cross{u}")
+            nc.vector.scalar_tensor_tensor(
+                part(cross[:], u), part(log_mu[:], u), -2.0, part(seen_t[k][:], u), ALU.mult, ALU.mult
+            )
+            if u == 4:
+                add_turned(u, own[k], True, False)
+                add_turned(u, mu2[k][:], False, False)
+            add_turned(u, cross[:], False, True)
+
+        def leave(u, copy):
+            k, halves, tag = units[u]
+            n = len(halves)
+            res = keep.tile([P, n * CH], F32, name=f"res{u}")
+            copy(res[:], total[u][:, 0 : n * CH])
+            nc.sync.dma_start(
+                out_rows[:, halves[0] : halves[0] + n, k * CH : (k + 1) * CH], res[:].rearrange("p (h j) -> p h j", h=n)
+            )
+
+        expected(0)
+        expected(1)
+        expected(2)
+        cross_term(0)
+        expected(3)
+        for u in range(1, 5):
+            cross_term(u)
+        for u, copy in enumerate([nc.scalar.copy, nc.scalar.copy, nc.vector.tensor_copy, nc.scalar.copy, nc.vector.tensor_copy]):
+            leave(u, copy)

@@ -50,11 +50,7 @@ def tile_picked_yrenew_dev_p_kernel(tc, x_words, x_scales, w1, inc, offs, out):
         for k in range(NCH):
             nc.sync.dma_start(seen[:, :, PAD + k * CH : PAD + (k + 1) * CH], inc_rows[:, :, k * CH : (k + 1) * CH])
 
-        for q in range(4):
-            nc.sync.dma_start(
-                scale_win[32 * q : 32 * q + 4, :].bitcast(I32),
-                x_scales[0, 4 * q : 4 * q + 4, :].bitcast(I32),
-            )
+        nc.sync.dma_start(scale_win[0:P:8, :].bitcast(I32), x_scales[0].bitcast(I32))
 
         w_raw = keep.tile([P, 4, N], F32, name="w_raw")
         nc.sync.dma_start(w_raw[:], w1.rearrange("(p j) m -> p j m", j=4))
@@ -78,6 +74,7 @@ def tile_picked_yrenew_dev_p_kernel(tc, x_words, x_scales, w1, inc, offs, out):
             nc.scalar.activation(ls[:], st[:], ACT.Ln, bias=0.05 / math.e, scale=1.0 / math.e)
             log_seen.append(ls)
 
+        for k in range(NCH):
             lo = PAD + k * CH - (1 if k == 0 else 0)
             hi = PAD + (k + 1) * CH
             nc.vector.scalar_tensor_tensor(
@@ -109,8 +106,12 @@ def tile_picked_yrenew_dev_p_kernel(tc, x_words, x_scales, w1, inc, offs, out):
         exp_cap = keep.tile([P, 1], F32, name="exp_cap")
         nc.scalar.activation(exp_cap[:], log_seen[NCH - 1][:, 0:1], ACT.Exp, bias=CAP, scale=0.0)
 
+        picked_rows = keep.tile([P, S], U8, name="picked_rows", align_bytes=64)
+        nc.vector.tensor_copy(picked_rows[:], scale_win[:].indirect(offsets[:]))
         picked_scales = keep.tile([P, S], U8, name="picked_scales", align_bytes=64)
-        nc.vector.tensor_copy(picked_scales[:], scale_win[:].indirect(offsets[:]))
+        nc.gpsimd.memset(picked_scales[:].bitcast(I32), 0)
+        for r in range(4):
+            nc.sync.dma_start(picked_scales[r:P:32, :].bitcast(I32), picked_rows[8 * r : P : 32, :].bitcast(I32))
         picked = []
         for d in range(2):
             t = keep.tile([P, HALF], U32, name=f"picked{d}", align_bytes=64)

@@ -18,11 +18,14 @@ ALU = mybir.AluOpType
 ACT = mybir.ActivationFunctionType
 
 P = 128
-HALF = 512
-CH = 256
-NCH = S // CH
+DAYS = 512
+HALF = DAYS // 2
+BLOCKS = DAYS // P
+CHUNKS = [(d, h) for d in range(S // DAYS) for h in range(N // P)]
 PAD = 8
 CAP = 32.0
+EARLY = 2
+PIECES = [(c, 0, DAYS) for c in range(EARLY)] + [(c, j, HALF) for c in range(EARLY, len(CHUNKS)) for j in (0, HALF)]
 
 
 def tile_picked_yrenew_dev_p_kernel(tc, x_words, x_scales, w1, inc, offs, out):
@@ -31,11 +34,17 @@ def tile_picked_yrenew_dev_p_kernel(tc, x_words, x_scales, w1, inc, offs, out):
         keep = ctx.enter_context(tc.tile_pool(name="keep", bufs=1))
         psum = ctx.enter_context(tc.psum_pool(name="psum", bufs=1))
 
+        def block(b):
+            return slice(b * P, (b + 1) * P)
+
+        def add_transposed(dst, src, start, stop):
+            nc.tensor.matmul(dst, lhsT=src, rhs=ident[:], is_transpose=True, start=start, stop=stop)
+
         offsets = keep.tile([P, S // 16], U16, name="offsets")
         nc.sync.dma_start(offsets[:], offs)
 
-        scale_win = keep.tile([P, T], U8, name="scale_win", align_bytes=64)
-        nc.vector.memset(scale_win[:].bitcast(I32), 0)
+        scale_window = keep.tile([P, T], U8, name="scale_window", align_bytes=64)
+        nc.vector.memset(scale_window[:].bitcast(I32), 0)
 
         one = keep.tile([P, 1], F32, name="one")
         nc.gpsimd.memset(one[:], 1.0)
@@ -44,182 +53,149 @@ def tile_picked_yrenew_dev_p_kernel(tc, x_words, x_scales, w1, inc, offs, out):
         ident = keep.tile([P, P], F32, name="ident")
         make_identity(nc, ident[:])
 
-        seen = keep.tile([P, 2, PAD + S], F32, name="seen", align_bytes=64)
-        nc.vector.memset(seen[:, :, 0:PAD], 0.0)
-        inc_rows = inc.rearrange("(h p) j -> p h j", h=2)
-        for k in range(NCH):
-            nc.sync.dma_start(seen[:, :, PAD + k * CH : PAD + (k + 1) * CH], inc_rows[:, :, k * CH : (k + 1) * CH])
+        seen = [keep.tile([P, PAD + S], F32, name=f"seen{h}", align_bytes=64) for h in range(N // P)]
+        for rows in seen:
+            nc.vector.memset(rows[:, 0:PAD], 0.0)
+        for d, h in CHUNKS:
+            nc.sync.dma_start(seen[h][:, PAD + d * DAYS : PAD + (d + 1) * DAYS], inc[block(h), d * DAYS : (d + 1) * DAYS])
 
-        nc.sync.dma_start(scale_win[0:P:8, :].bitcast(I32), x_scales[0].bitcast(I32))
+        nc.sync.dma_start(scale_window[0:P:8, :].bitcast(I32), x_scales[0].bitcast(I32))
 
         w_raw = keep.tile([P, 4, N], F32, name="w_raw")
-        nc.sync.dma_start(w_raw[:], w1.rearrange("(p j) m -> p j m", j=4))
+        nc.sync.dma_start(w_raw[:], w1.rearrange("(p t) m -> p t m", t=4))
 
-        word_win = keep.tile([P, T], I32, name="word_win", tag="word_win", align_bytes=64)
-        nc.sync.dma_start(word_win[:], x_words[0].rearrange("p n t -> p (n t)").bitcast(I32))
+        word_window = keep.tile([P, T], I32, name="word_window", tag="word_window", align_bytes=64)
+        nc.sync.dma_start(word_window[:], x_words[0].rearrange("p n t -> p (n t)").bitcast(I32))
 
-        def turned(b, h):
-            return slice(b * N + h * P, b * N + (h + 1) * P)
-
-        pair = keep.tile([P, 2, PAD + S], F32, name="pair", align_bytes=64)
-        seen_t, log_seen, conv = [], [], []
-        for k in range(NCH):
-            st = psum.tile([P, 2 * N], F32, name=f"seen_t{k}", tag=f"seen_t{k}")
-            for b in range(2):
-                for h in range(2):
-                    j0 = PAD + k * CH + b * P
-                    nc.tensor.transpose(st[:, turned(b, h)], seen[:, h, j0 : j0 + P], ident[:])
-            seen_t.append(st)
-            ls = keep.tile([P, 2 * N], F32, name=f"log_seen{k}")
-            nc.scalar.activation(ls[:], st[:], ACT.Ln, bias=0.05 / math.e, scale=1.0 / math.e)
-            log_seen.append(ls)
-
-        for k in range(NCH):
-            lo = PAD + k * CH - (1 if k == 0 else 0)
-            hi = PAD + (k + 1) * CH
-            nc.vector.scalar_tensor_tensor(
-                pair[:, :, lo:hi], seen[:, :, lo - 2 : hi - 2], 1.5, seen[:, :, lo - 1 : hi - 1], ALU.mult, ALU.add
-            )
-            ct = psum.tile([P, 2 * N], F32, name=f"conv_t{k}", tag=f"work{k}")
-            for b in range(2):
-                for h in range(2):
-                    j0 = PAD + k * CH + b * P
-                    for back in range(2):
-                        nc.tensor.matmul(
-                            ct[:, turned(b, h)],
-                            lhsT=pair[:, h, j0 - back : j0 - back + P],
-                            rhs=ident[:],
-                            is_transpose=True,
-                            start=(back == 0),
-                            stop=(back == 1),
-                        )
-            cs = keep.tile([P, 2 * N], F32, name=f"conv{k}")
-            nc.scalar.activation(cs[:], ct[:], ACT.Copy, scale=2.0 * 1.3 * 0.2 / CAP)
-            conv.append(cs)
-
-        w_bf = keep.tile([P, N, 4], BF16, name="w_bf", align_bytes=64)
-        nc.scalar.copy(w_bf[:], w_raw[:].rearrange("p j m -> p m j"))
-        w_codes = keep.tile([P, N], U32, name="w_codes", align_bytes=64)
-        w_scales = keep.tile([P, N], U8, name="w_scales", align_bytes=64)
-        nc.vector.quantize_mx(w_codes[:].bitcast(FP8X4), w_scales[:], w_bf[:].rearrange("p m j -> p (m j)"))
+        seen_turned, log_seen = [], []
+        for c, (d, h) in enumerate(CHUNKS):
+            turned = psum.tile([P, DAYS], F32, name=f"seen_turned{c}", tag=f"bank{len(CHUNKS) + c}")
+            for b in range(BLOCKS):
+                j0 = PAD + d * DAYS + b * P
+                nc.tensor.transpose(turned[:, block(b)], seen[h][:, j0 : j0 + P], ident[:])
+            seen_turned.append(turned)
+            log_minus_one = keep.tile([P, DAYS], F32, name=f"log_seen{c}")
+            nc.scalar.activation(log_minus_one[:], turned[:], ACT.Ln, bias=0.05 / math.e, scale=1.0 / math.e)
+            log_seen.append(log_minus_one)
 
         exp_cap = keep.tile([P, 1], F32, name="exp_cap")
-        nc.scalar.activation(exp_cap[:], log_seen[NCH - 1][:, 0:1], ACT.Exp, bias=CAP, scale=0.0)
+        nc.scalar.activation(exp_cap[:], log_seen[-1][:, 0:1], ACT.Exp, bias=CAP, scale=0.0)
+
+        pair = [keep.tile([P, PAD + S], F32, name=f"pair{h}", align_bytes=64) for h in range(N // P)]
+        conv = []
+        for c, (d, h) in enumerate(CHUNKS):
+            lo = PAD + d * DAYS - (1 if d == 0 else 0)
+            hi = PAD + (d + 1) * DAYS
+            nc.vector.scalar_tensor_tensor(
+                pair[h][:, lo:hi], seen[h][:, lo - 2 : hi - 2], 1.5, seen[h][:, lo - 1 : hi - 1], ALU.mult, ALU.add
+            )
+            conv_turned = psum.tile([P, DAYS], F32, name=f"conv_turned{c}", tag=f"bank{c}")
+            for b in range(BLOCKS):
+                j0 = PAD + d * DAYS + b * P
+                add_transposed(conv_turned[:, block(b)], pair[h][:, j0 : j0 + P], True, False)
+                add_transposed(conv_turned[:, block(b)], pair[h][:, j0 - 1 : j0 - 1 + P], False, True)
+            scaled = keep.tile([P, DAYS], F32, name=f"conv{c}")
+            nc.scalar.activation(scaled[:], conv_turned[:], ACT.Copy, scale=2.0 * 1.3 * 0.2 / CAP)
+            conv.append(scaled)
+
+        w_bf16 = keep.tile([P, N, 4], BF16, name="w_bf16", align_bytes=64)
+        nc.vector.tensor_copy(w_bf16[:], w_raw[:].rearrange("p t m -> p m t"))
+        w_codes = keep.tile([P, N], U32, name="w_codes", align_bytes=64)
+        w_scales = keep.tile([P, N], U8, name="w_scales", align_bytes=64)
+        nc.vector.quantize_mx(w_codes[:].bitcast(FP8X4), w_scales[:], w_bf16[:].rearrange("p m t -> p (m t)"))
+
+        seen_for_cross = seen_turned[:EARLY]
+        for c in range(EARLY, len(CHUNKS)):
+            copied = keep.tile([P, DAYS], F32, name=f"seen_copied{c}")
+            nc.scalar.copy(copied[:], seen_turned[c][:])
+            seen_for_cross.append(copied)
 
         picked_rows = keep.tile([P, S], U8, name="picked_rows", align_bytes=64)
-        nc.vector.tensor_copy(picked_rows[:], scale_win[:].indirect(offsets[:]))
+        nc.vector.tensor_copy(picked_rows[:], scale_window[:].indirect(offsets[:]))
         picked_scales = keep.tile([P, S], U8, name="picked_scales", align_bytes=64)
         nc.gpsimd.memset(picked_scales[:].bitcast(I32), 0)
         for r in range(4):
             nc.sync.dma_start(picked_scales[r:P:32, :].bitcast(I32), picked_rows[8 * r : P : 32, :].bitcast(I32))
-        picked = []
-        for d in range(2):
-            t = keep.tile([P, HALF], U32, name=f"picked{d}", align_bytes=64)
-            nc.vector.tensor_copy(
-                t[:], word_win[:].bitcast(U32).indirect(offsets[:, d * HALF // 16 : (d + 1) * HALF // 16])
-            )
-            picked.append(t)
 
-        gain, capped = [], []
-        for k in range(NCH):
-            y = psum.tile([P, 2 * N], F32, name=f"y{k}", tag=f"work{k}")
-            for b in range(2):
-                j0 = k * CH + b * P
+        picked_words = []
+        for d in range(S // DAYS):
+            words = keep.tile([P, DAYS], U32, name=f"picked_words{d}", align_bytes=64)
+            entries = offsets[:, d * DAYS // 16 : (d + 1) * DAYS // 16]
+            nc.vector.tensor_copy(words[:], word_window[:].bitcast(U32).indirect(entries))
+            picked_words.append(words)
+
+        capped, gain = [], []
+        for c, (d, h) in enumerate(CHUNKS):
+            y = psum.tile([P, DAYS], F32, name=f"y{c}", tag=f"bank{c}")
+            for b in range(BLOCKS):
                 nc.tensor.matmul_mx(
-                    y[:, b * N : (b + 1) * N],
-                    lhsT=picked[j0 // HALF][:, j0 % HALF : j0 % HALF + P].bitcast(FP8X4),
-                    lhsT_scale=picked_scales[:, j0 : j0 + P],
-                    rhs=w_codes[:].bitcast(FP8X4),
-                    rhs_scale=w_scales[:],
+                    y[:, block(b)],
+                    lhsT=picked_words[d][:, block(b)].bitcast(FP8X4),
+                    lhsT_scale=picked_scales[:, block(d * BLOCKS + b)],
+                    rhs=w_codes[:, block(h)].bitcast(FP8X4),
+                    rhs_scale=w_scales[:, block(h)],
                     start=True,
                     stop=True,
                 )
-            grown = keep.tile([P, 2 * N], F32, name=f"grown{k}")
+            grown = keep.tile([P, DAYS], F32, name=f"grown{c}")
             nc.scalar.activation(grown[:], y[:], ACT.Exp, bias=zero[:])
-            cp = keep.tile([P, 2 * N], F32, name=f"capped{k}")
-            nc.gpsimd.tensor_scalar(cp[:], grown[:], exp_cap[:], 0.0, ALU.min, ALU.max)
-            capped.append(cp)
-            g = keep.tile([P, 2 * N], F32, name=f"gain{k}")
-            nc.vector.scalar_tensor_tensor(g[:], y[:], CAP, conv[k][:], ALU.max, ALU.mult)
-            gain.append(g)
+            limited = keep.tile([P, DAYS], F32, name=f"capped{c}")
+            nc.gpsimd.tensor_scalar(limited[:], grown[:], exp_cap[:], 0.0, ALU.min, ALU.max)
+            capped.append(limited)
+            factor = keep.tile([P, DAYS], F32, name=f"gain{c}")
+            nc.vector.scalar_tensor_tensor(factor[:], y[:], CAP, conv[c][:], ALU.max, ALU.mult)
+            gain.append(factor)
 
-        late = keep.tile([P, 2, 2 * N], F32, name="own_late", tag="word_win", align_bytes=64)
-        own = []
-        for k in range(NCH):
-            if k < 2:
-                early = keep.tile([P, 2 * N], F32, name=f"own{k}")
-                o = early[:]
-            else:
-                o = late[:, k - 2, :]
-            nc.vector.scalar_tensor_tensor(o, log_seen[k][:], 2.0, seen_t[k][:], ALU.mult, ALU.mult)
-            own.append(o)
+        own_early = keep.tile([P, EARLY, DAYS], F32, name="own_early")
+        own_late = keep.tile([P, len(CHUNKS) - EARLY, DAYS], F32, name="own_late", tag="word_window", align_bytes=64)
+        own = [own_early[:, c, :] if c < EARLY else own_late[:, c - EARLY, :] for c in range(len(CHUNKS))]
+        for c in range(len(CHUNKS)):
+            nc.vector.scalar_tensor_tensor(own[c], log_seen[c][:], 2.0, seen_turned[c][:], ALU.mult, ALU.mult)
 
-        units = [(0, (0, 1), "work0"), (1, (0, 1), "work1"), (2, (0, 1), "work2"), (3, (0,), "work3"), (3, (1,), "seen_t0")]
+        def add_term(i, term, j0, days, first, last):
+            blocks = range(j0 // P, (j0 + days) // P)
+            for b in blocks:
+                dst = total[i][:, block(b - PIECES[i][1] // P)]
+                add_transposed(dst, term[:, block(b)], first and b == blocks[0], last and b == blocks[-1])
 
-        def part(ap, u):
-            halves = units[u][1]
-            if len(halves) == 2:
-                return ap
-            return ap.rearrange("p (b h m) -> p b h m", b=2, h=2)[:, :, halves[0], :]
+        total = []
+        for i, (c, j0, days) in enumerate(PIECES):
+            bank = c if j0 == 0 else len(CHUNKS) + c
+            total.append(psum.tile([P, days], F32, name=f"total{i}", tag=f"bank{bank}"))
+            add_term(i, own[c], j0, days, True, False)
 
-        total = {}
+        mu2 = [keep.tile([P, DAYS], F32, name=f"mu2_{c}") for c in range(len(CHUNKS))]
 
-        def add_turned(u, term, first, last):
-            k, halves, tag = units[u]
-            if first:
-                total[u] = psum.tile([P, 2 * CH], F32, name=f"total{u}", tag=tag)
-            for i, h in enumerate(halves):
-                for b in range(2):
-                    nc.tensor.matmul(
-                        total[u][:, i * CH + b * P : i * CH + (b + 1) * P],
-                        lhsT=term[:, turned(b, h)],
-                        rhs=ident[:],
-                        is_transpose=True,
-                        start=(first and i == 0 and b == 0),
-                        stop=(last and i == len(halves) - 1 and b == 1),
+        def expected(c):
+            for j0 in (0, HALF):
+                cols = slice(j0, j0 + HALF)
+                soft = keep.tile([P, HALF], F32, name=f"soft{c}_{j0}")
+                nc.scalar.activation(soft[:], capped[c][:, cols], ACT.Ln, bias=1.0)
+                nc.vector.tensor_mul(mu2[c][:, cols], soft[:], gain[c][:, cols])
+                piece = [i for i, (pc, pj, days) in enumerate(PIECES) if pc == c and pj <= j0 < pj + days][0]
+                add_term(piece, mu2[c], j0, HALF, False, False)
+
+        def cross_terms(c):
+            for i, (pc, j0, days) in enumerate(PIECES):
+                if pc == c:
+                    cols = slice(j0, j0 + days)
+                    log_mu = keep.tile([P, DAYS], F32, name=f"log_mu{i}")
+                    nc.scalar.activation(log_mu[:, cols], mu2[c][:, cols], ACT.Ln, bias=0.05, scale=0.5)
+                    cross = keep.tile([P, DAYS], F32, name=f"cross{i}")
+                    nc.vector.scalar_tensor_tensor(
+                        cross[:, cols], log_mu[:, cols], -2.0, seen_for_cross[c][:, cols], ALU.mult, ALU.mult
                     )
-
-        for u in range(4):
-            add_turned(u, own[units[u][0]], True, False)
-
-        out_rows = out.rearrange("(h p) j -> p h j", h=2)
-        mu2 = {}
-
-        def expected(k):
-            soft = keep.tile([P, 2 * N], F32, name=f"soft{k}")
-            nc.scalar.activation(soft[:], capped[k][:], ACT.Ln, bias=1.0)
-            mu2[k] = keep.tile([P, 2 * N], F32, name=f"mu2_{k}")
-            nc.vector.tensor_mul(mu2[k][:], soft[:], gain[k][:])
-            add_turned(k, mu2[k][:], False, False)
-
-        def cross_term(u):
-            k = units[u][0]
-            log_mu = keep.tile([P, 2 * N], F32, name=f"log_mu{u}")
-            nc.scalar.activation(part(log_mu[:], u), part(mu2[k][:], u), ACT.Ln, bias=0.05, scale=0.5)
-            cross = keep.tile([P, 2 * N], F32, name=f"cross{u}")
-            nc.vector.scalar_tensor_tensor(
-                part(cross[:], u), part(log_mu[:], u), -2.0, part(seen_t[k][:], u), ALU.mult, ALU.mult
-            )
-            if u == 4:
-                add_turned(u, own[k], True, False)
-                add_turned(u, mu2[k][:], False, False)
-            add_turned(u, cross[:], False, True)
-
-        def leave(u, copy):
-            k, halves, tag = units[u]
-            n = len(halves)
-            res = keep.tile([P, n * CH], F32, name=f"res{u}")
-            copy(res[:], total[u][:, 0 : n * CH])
-            nc.sync.dma_start(
-                out_rows[:, halves[0] : halves[0] + n, k * CH : (k + 1) * CH], res[:].rearrange("p (h j) -> p h j", h=n)
-            )
+                    add_term(i, cross, j0, days, False, True)
 
         expected(0)
-        expected(1)
-        expected(2)
-        cross_term(0)
-        expected(3)
-        for u in range(1, 5):
-            cross_term(u)
-        for u, copy in enumerate([nc.scalar.copy, nc.scalar.copy, nc.vector.tensor_copy, nc.scalar.copy, nc.vector.tensor_copy]):
-            leave(u, copy)
+        for c in range(1, len(CHUNKS)):
+            expected(c)
+            cross_terms(c - 1)
+        cross_terms(len(CHUNKS) - 1)
+
+        for i, (c, j0, days) in enumerate(PIECES):
+            d, h = CHUNKS[c]
+            result = keep.tile([P, days], F32, name=f"result{i}")
+            copy = nc.scalar.copy if j0 == 0 else nc.vector.tensor_copy
+            copy(result[:], total[i][:])
+            nc.sync.dma_start(out[block(h), d * DAYS + j0 : d * DAYS + j0 + days], result[:])

@@ -24,8 +24,8 @@ BLOCKS = DAYS // P
 CHUNKS = [(d, h) for d in range(S // DAYS) for h in range(N // P)]
 PAD = 8
 CAP = 32.0
-EARLY = 2
-PIECES = [(c, 0, DAYS) for c in range(EARLY)] + [(c, j, HALF) for c in range(EARLY, len(CHUNKS)) for j in (0, HALF)]
+WHOLE = 2
+PIECES = [(c, 0, DAYS) for c in range(WHOLE)] + [(c, j, HALF) for c in range(WHOLE, len(CHUNKS)) for j in (0, HALF)]
 
 
 def tile_picked_yrenew_dev_p_kernel(tc, x_words, x_scales, w1, inc, offs, out):
@@ -46,6 +46,8 @@ def tile_picked_yrenew_dev_p_kernel(tc, x_words, x_scales, w1, inc, offs, out):
         scale_window = keep.tile([P, T], U8, name="scale_window", align_bytes=64)
         nc.vector.memset(scale_window[:].bitcast(I32), 0)
 
+        nc.sync.dma_start(scale_window[0:P:8, :].bitcast(I32), x_scales[0].bitcast(I32))
+
         one = keep.tile([P, 1], F32, name="one")
         nc.gpsimd.memset(one[:], 1.0)
         zero = keep.tile([P, 1], F32, name="zero")
@@ -59,13 +61,18 @@ def tile_picked_yrenew_dev_p_kernel(tc, x_words, x_scales, w1, inc, offs, out):
         for d, h in CHUNKS:
             nc.sync.dma_start(seen[h][:, PAD + d * DAYS : PAD + (d + 1) * DAYS], inc[block(h), d * DAYS : (d + 1) * DAYS])
 
-        nc.sync.dma_start(scale_window[0:P:8, :].bitcast(I32), x_scales[0].bitcast(I32))
-
         w_raw = keep.tile([P, 4, N], F32, name="w_raw")
         nc.sync.dma_start(w_raw[:], w1.rearrange("(p t) m -> p t m", t=4))
 
         word_window = keep.tile([P, T], I32, name="word_window", tag="word_window", align_bytes=64)
         nc.sync.dma_start(word_window[:], x_words[0].rearrange("p n t -> p (n t)").bitcast(I32))
+
+        picked_rows = keep.tile([P, S], U8, name="picked_rows", align_bytes=64)
+        nc.vector.tensor_copy(picked_rows[:], scale_window[:].indirect(offsets[:]))
+        picked_scales = keep.tile([P, S], U8, name="picked_scales", align_bytes=64)
+        nc.gpsimd.memset(picked_scales[:].bitcast(I32), 0)
+        for r in range(4):
+            nc.sync.dma_start(picked_scales[r:P:32, :].bitcast(I32), picked_rows[8 * r : P : 32, :].bitcast(I32))
 
         seen_turned, log_seen = [], []
         for c, (d, h) in enumerate(CHUNKS):
@@ -81,19 +88,22 @@ def tile_picked_yrenew_dev_p_kernel(tc, x_words, x_scales, w1, inc, offs, out):
         exp_cap = keep.tile([P, 1], F32, name="exp_cap")
         nc.scalar.activation(exp_cap[:], log_seen[-1][:, 0:1], ACT.Exp, bias=CAP, scale=0.0)
 
-        pair = [keep.tile([P, PAD + S], F32, name=f"pair{h}", align_bytes=64) for h in range(N // P)]
         conv = []
         for c, (d, h) in enumerate(CHUNKS):
-            lo = PAD + d * DAYS - (1 if d == 0 else 0)
-            hi = PAD + (d + 1) * DAYS
+            j0 = PAD + d * DAYS
+            pair = keep.tile([P, 1 + DAYS], F32, name=f"pair{c}")
             nc.vector.scalar_tensor_tensor(
-                pair[h][:, lo:hi], seen[h][:, lo - 2 : hi - 2], 1.5, seen[h][:, lo - 1 : hi - 1], ALU.mult, ALU.add
+                pair[:], seen[h][:, j0 - 3 : j0 + DAYS - 2], 1.5, seen[h][:, j0 - 2 : j0 + DAYS - 1], ALU.mult, ALU.add
             )
+            terms = [pair[:, 1:], pair[:, :DAYS]]
+            if d > 0:
+                summed = keep.tile([P, DAYS], F32, name=f"summed{c}")
+                nc.vector.tensor_add(summed[:], terms[0], terms[1])
+                terms = [summed[:]]
             conv_turned = psum.tile([P, DAYS], F32, name=f"conv_turned{c}", tag=f"bank{c}")
             for b in range(BLOCKS):
-                j0 = PAD + d * DAYS + b * P
-                add_transposed(conv_turned[:, block(b)], pair[h][:, j0 : j0 + P], True, False)
-                add_transposed(conv_turned[:, block(b)], pair[h][:, j0 - 1 : j0 - 1 + P], False, True)
+                for i, term in enumerate(terms):
+                    add_transposed(conv_turned[:, block(b)], term[:, block(b)], i == 0, i == len(terms) - 1)
             scaled = keep.tile([P, DAYS], F32, name=f"conv{c}")
             nc.scalar.activation(scaled[:], conv_turned[:], ACT.Copy, scale=2.0 * 1.3 * 0.2 / CAP)
             conv.append(scaled)
@@ -104,18 +114,11 @@ def tile_picked_yrenew_dev_p_kernel(tc, x_words, x_scales, w1, inc, offs, out):
         w_scales = keep.tile([P, N], U8, name="w_scales", align_bytes=64)
         nc.vector.quantize_mx(w_codes[:].bitcast(FP8X4), w_scales[:], w_bf16[:].rearrange("p m t -> p (m t)"))
 
-        seen_for_cross = seen_turned[:EARLY]
-        for c in range(EARLY, len(CHUNKS)):
+        seen_for_cross = seen_turned[:WHOLE]
+        for c in range(WHOLE, len(CHUNKS)):
             copied = keep.tile([P, DAYS], F32, name=f"seen_copied{c}")
             nc.scalar.copy(copied[:], seen_turned[c][:])
             seen_for_cross.append(copied)
-
-        picked_rows = keep.tile([P, S], U8, name="picked_rows", align_bytes=64)
-        nc.vector.tensor_copy(picked_rows[:], scale_window[:].indirect(offsets[:]))
-        picked_scales = keep.tile([P, S], U8, name="picked_scales", align_bytes=64)
-        nc.gpsimd.memset(picked_scales[:].bitcast(I32), 0)
-        for r in range(4):
-            nc.sync.dma_start(picked_scales[r:P:32, :].bitcast(I32), picked_rows[8 * r : P : 32, :].bitcast(I32))
 
         picked_words = []
         for d in range(S // DAYS):
@@ -146,11 +149,9 @@ def tile_picked_yrenew_dev_p_kernel(tc, x_words, x_scales, w1, inc, offs, out):
             nc.vector.scalar_tensor_tensor(factor[:], y[:], CAP, conv[c][:], ALU.max, ALU.mult)
             gain.append(factor)
 
-        own_early = keep.tile([P, EARLY, DAYS], F32, name="own_early")
-        own_late = keep.tile([P, len(CHUNKS) - EARLY, DAYS], F32, name="own_late", tag="word_window", align_bytes=64)
-        own = [own_early[:, c, :] if c < EARLY else own_late[:, c - EARLY, :] for c in range(len(CHUNKS))]
+        own = keep.tile([P, len(CHUNKS), DAYS], F32, name="own", tag="word_window", align_bytes=64)
         for c in range(len(CHUNKS)):
-            nc.vector.scalar_tensor_tensor(own[c], log_seen[c][:], 2.0, seen_turned[c][:], ALU.mult, ALU.mult)
+            nc.vector.scalar_tensor_tensor(own[:, c, :], log_seen[c][:], 2.0, seen_turned[c][:], ALU.mult, ALU.mult)
 
         def add_term(i, term, j0, days, first, last):
             blocks = range(j0 // P, (j0 + days) // P)
@@ -162,7 +163,7 @@ def tile_picked_yrenew_dev_p_kernel(tc, x_words, x_scales, w1, inc, offs, out):
         for i, (c, j0, days) in enumerate(PIECES):
             bank = c if j0 == 0 else len(CHUNKS) + c
             total.append(psum.tile([P, days], F32, name=f"total{i}", tag=f"bank{bank}"))
-            add_term(i, own[c], j0, days, True, False)
+            add_term(i, own[:, c, :], j0, days, True, False)
 
         mu2 = [keep.tile([P, DAYS], F32, name=f"mu2_{c}") for c in range(len(CHUNKS))]
 

import math
from contextlib import ExitStack

import concourse.mybir as mybir
from concourse.masks import make_identity

K, T, S, N = 512, 4096, 1024, 256
FLOPS = 2 * K * N * S

F32 = mybir.dt.float32
BF16 = mybir.dt.bfloat16
I32 = mybir.dt.int32
U32 = mybir.dt.uint32
U16 = mybir.dt.uint16
U8 = mybir.dt.uint8
FP8X4 = mybir.dt.float8_e4m3fn_x4
ALU = mybir.AluOpType
ACT = mybir.ActivationFunctionType

P = 128
DAYS = 512
HALF = DAYS // 2
BLOCKS = DAYS // P
CHUNKS = [(d, h) for d in range(S // DAYS) for h in range(N // P)]
PAD = 8
CAP = 32.0
WHOLE = 2
PIECES = [(c, 0, DAYS) for c in range(WHOLE)] + [(c, j, HALF) for c in range(WHOLE, len(CHUNKS)) for j in (0, HALF)]


def tile_picked_yrenew_dev_p_kernel(tc, x_words, x_scales, w1, inc, offs, out):
    nc = tc.nc
    with ExitStack() as ctx:
        keep = ctx.enter_context(tc.tile_pool(name="keep", bufs=1))
        psum = ctx.enter_context(tc.psum_pool(name="psum", bufs=1))

        def block(b):
            return slice(b * P, (b + 1) * P)

        def add_transposed(dst, src, start, stop):
            nc.tensor.matmul(dst, lhsT=src, rhs=ident[:], is_transpose=True, start=start, stop=stop)

        offsets = keep.tile([P, S // 16], U16, name="offsets")
        nc.sync.dma_start(offsets[:], offs)

        scale_window = keep.tile([P, T], U8, name="scale_window", align_bytes=64)
        nc.vector.memset(scale_window[:].bitcast(I32), 0)

        nc.sync.dma_start(scale_window[0:P:8, :].bitcast(I32), x_scales[0].bitcast(I32))

        one = keep.tile([P, 1], F32, name="one")
        nc.gpsimd.memset(one[:], 1.0)
        zero = keep.tile([P, 1], F32, name="zero")
        nc.scalar.activation(zero[:], one[:], ACT.Ln)
        ident = keep.tile([P, P], F32, name="ident")
        make_identity(nc, ident[:])

        seen = [keep.tile([P, PAD + S], F32, name=f"seen{h}", align_bytes=64) for h in range(N // P)]
        for rows in seen:
            nc.vector.memset(rows[:, 0:PAD], 0.0)
        for d, h in CHUNKS:
            nc.sync.dma_start(seen[h][:, PAD + d * DAYS : PAD + (d + 1) * DAYS], inc[block(h), d * DAYS : (d + 1) * DAYS])

        w_raw = keep.tile([P, 4, N], F32, name="w_raw")
        nc.sync.dma_start(w_raw[:], w1.rearrange("(p t) m -> p t m", t=4))

        word_window = keep.tile([P, T], I32, name="word_window", tag="word_window", align_bytes=64)
        nc.sync.dma_start(word_window[:], x_words[0].rearrange("p n t -> p (n t)").bitcast(I32))

        picked_rows = keep.tile([P, S], U8, name="picked_rows", align_bytes=64)
        nc.vector.tensor_copy(picked_rows[:], scale_window[:].indirect(offsets[:]))
        picked_scales = keep.tile([P, S], U8, name="picked_scales", align_bytes=64)
        nc.gpsimd.memset(picked_scales[:].bitcast(I32), 0)
        for r in range(4):
            nc.sync.dma_start(picked_scales[r:P:32, :].bitcast(I32), picked_rows[8 * r : P : 32, :].bitcast(I32))

        seen_turned, log_seen = [], []
        for c, (d, h) in enumerate(CHUNKS):
            turned = psum.tile([P, DAYS], F32, name=f"seen_turned{c}", tag=f"bank{len(CHUNKS) + c}")
            for b in range(BLOCKS):
                j0 = PAD + d * DAYS + b * P
                nc.tensor.transpose(turned[:, block(b)], seen[h][:, j0 : j0 + P], ident[:])
            seen_turned.append(turned)
            log_minus_one = keep.tile([P, DAYS], F32, name=f"log_seen{c}")
            nc.scalar.activation(log_minus_one[:], turned[:], ACT.Ln, bias=0.05 / math.e, scale=1.0 / math.e)
            log_seen.append(log_minus_one)

        exp_cap = keep.tile([P, 1], F32, name="exp_cap")
        nc.scalar.activation(exp_cap[:], log_seen[-1][:, 0:1], ACT.Exp, bias=CAP, scale=0.0)

        conv = []
        for c, (d, h) in enumerate(CHUNKS):
            j0 = PAD + d * DAYS
            pair = keep.tile([P, 1 + DAYS], F32, name=f"pair{c}")
            nc.vector.scalar_tensor_tensor(
                pair[:], seen[h][:, j0 - 3 : j0 + DAYS - 2], 1.5, seen[h][:, j0 - 2 : j0 + DAYS - 1], ALU.mult, ALU.add
            )
            terms = [pair[:, 1:], pair[:, :DAYS]]
            if d > 0:
                summed = keep.tile([P, DAYS], F32, name=f"summed{c}")
                nc.vector.tensor_add(summed[:], terms[0], terms[1])
                terms = [summed[:]]
            conv_turned = psum.tile([P, DAYS], F32, name=f"conv_turned{c}", tag=f"bank{c}")
            for b in range(BLOCKS):
                for i, term in enumerate(terms):
                    add_transposed(conv_turned[:, block(b)], term[:, block(b)], i == 0, i == len(terms) - 1)
            scaled = keep.tile([P, DAYS], F32, name=f"conv{c}")
            nc.scalar.activation(scaled[:], conv_turned[:], ACT.Copy, scale=2.0 * 1.3 * 0.2 / CAP)
            conv.append(scaled)

        w_bf16 = keep.tile([P, N, 4], BF16, name="w_bf16", align_bytes=64)
        nc.vector.tensor_copy(w_bf16[:], w_raw[:].rearrange("p t m -> p m t"))
        w_codes = keep.tile([P, N], U32, name="w_codes", align_bytes=64)
        w_scales = keep.tile([P, N], U8, name="w_scales", align_bytes=64)
        nc.vector.quantize_mx(w_codes[:].bitcast(FP8X4), w_scales[:], w_bf16[:].rearrange("p m t -> p (m t)"))

        seen_for_cross = seen_turned[:WHOLE]
        for c in range(WHOLE, len(CHUNKS)):
            copied = keep.tile([P, DAYS], F32, name=f"seen_copied{c}")
            nc.scalar.copy(copied[:], seen_turned[c][:])
            seen_for_cross.append(copied)

        picked_words = []
        for d in range(S // DAYS):
            words = keep.tile([P, DAYS], U32, name=f"picked_words{d}", align_bytes=64)
            entries = offsets[:, d * DAYS // 16 : (d + 1) * DAYS // 16]
            nc.vector.tensor_copy(words[:], word_window[:].bitcast(U32).indirect(entries))
            picked_words.append(words)

        capped, gain = [], []
        for c, (d, h) in enumerate(CHUNKS):
            y = psum.tile([P, DAYS], F32, name=f"y{c}", tag=f"bank{c}")
            for b in range(BLOCKS):
                nc.tensor.matmul_mx(
                    y[:, block(b)],
                    lhsT=picked_words[d][:, block(b)].bitcast(FP8X4),
                    lhsT_scale=picked_scales[:, block(d * BLOCKS + b)],
                    rhs=w_codes[:, block(h)].bitcast(FP8X4),
                    rhs_scale=w_scales[:, block(h)],
                    start=True,
                    stop=True,
                )
            grown = keep.tile([P, DAYS], F32, name=f"grown{c}")
            nc.scalar.activation(grown[:], y[:], ACT.Exp, bias=zero[:])
            limited = keep.tile([P, DAYS], F32, name=f"capped{c}")
            nc.gpsimd.tensor_scalar(limited[:], grown[:], exp_cap[:], 0.0, ALU.min, ALU.max)
            capped.append(limited)
            factor = keep.tile([P, DAYS], F32, name=f"gain{c}")
            nc.vector.scalar_tensor_tensor(factor[:], y[:], CAP, conv[c][:], ALU.max, ALU.mult)
            gain.append(factor)

        own = keep.tile([P, len(CHUNKS), DAYS], F32, name="own", tag="word_window", align_bytes=64)
        for c in range(len(CHUNKS)):
            nc.vector.scalar_tensor_tensor(own[:, c, :], log_seen[c][:], 2.0, seen_turned[c][:], ALU.mult, ALU.mult)

        def add_term(i, term, j0, days, first, last):
            blocks = range(j0 // P, (j0 + days) // P)
            for b in blocks:
                dst = total[i][:, block(b - PIECES[i][1] // P)]
                add_transposed(dst, term[:, block(b)], first and b == blocks[0], last and b == blocks[-1])

        total = []
        for i, (c, j0, days) in enumerate(PIECES):
            bank = c if j0 == 0 else len(CHUNKS) + c
            total.append(psum.tile([P, days], F32, name=f"total{i}", tag=f"bank{bank}"))
            add_term(i, own[:, c, :], j0, days, True, False)

        mu2 = [keep.tile([P, DAYS], F32, name=f"mu2_{c}") for c in range(len(CHUNKS))]

        def expected(c):
            for j0 in (0, HALF):
                cols = slice(j0, j0 + HALF)
                soft = keep.tile([P, HALF], F32, name=f"soft{c}_{j0}")
                nc.scalar.activation(soft[:], capped[c][:, cols], ACT.Ln, bias=1.0)
                nc.vector.tensor_mul(mu2[c][:, cols], soft[:], gain[c][:, cols])
                piece = [i for i, (pc, pj, days) in enumerate(PIECES) if pc == c and pj <= j0 < pj + days][0]
                add_term(piece, mu2[c], j0, HALF, False, False)

        def cross_terms(c):
            for i, (pc, j0, days) in enumerate(PIECES):
                if pc == c:
                    cols = slice(j0, j0 + days)
                    log_mu = keep.tile([P, DAYS], F32, name=f"log_mu{i}")
                    nc.scalar.activation(log_mu[:, cols], mu2[c][:, cols], ACT.Ln, bias=0.05, scale=0.5)
                    cross = keep.tile([P, DAYS], F32, name=f"cross{i}")
                    nc.vector.scalar_tensor_tensor(
                        cross[:, cols], log_mu[:, cols], -2.0, seen_for_cross[c][:, cols], ALU.mult, ALU.mult
                    )
                    add_term(i, cross, j0, days, False, True)

        expected(0)
        for c in range(1, len(CHUNKS)):
            expected(c)
            cross_terms(c - 1)
        cross_terms(len(CHUNKS) - 1)

        for i, (c, j0, days) in enumerate(PIECES):
            d, h = CHUNKS[c]
            result = keep.tile([P, days], F32, name=f"result{i}")
            copy = nc.scalar.copy if j0 == 0 else nc.vector.tensor_copy
            copy(result[:], total[i][:])
            nc.sync.dma_start(out[block(h), d * DAYS + j0 : d * DAYS + j0 + days], result[:])
